import numpy as np
import ml_dtypes


def mxq(x, axis, fmt="e4m3"):
    dtype, down = {"e4m3": (ml_dtypes.float8_e4m3fn, 7), "e5m2": (ml_dtypes.float8_e5m2, 14)}[fmt]
    v = np.moveaxis(np.asarray(x, np.float32).astype(ml_dtypes.bfloat16).astype(np.float64), axis, -1)
    blocks = v.reshape(v.shape[:-1] + (-1, 32))
    amax = np.abs(blocks).max(-1, keepdims=True)
    byte = np.maximum(np.where(amax > 0, np.frexp(amax)[1] - 1 + 127, 0) - down, 1)
    scale = np.exp2(byte - 127.0)
    codes = (blocks / scale).astype(np.float32).astype(dtype).astype(np.float64)
    return np.moveaxis((codes * scale).reshape(v.shape), -1, axis)


WIDE = False


def mx_kscale(k):
    if not WIDE:
        return np.ones(k)
    levels = np.array([10, -10, 5, -5, 0])
    if k % 512:
        return np.exp2(np.random.permutation(np.resize(levels, k // 32))).repeat(32)
    a = np.empty((k // 512, 16))
    for p in range(k // 512):
        a[p, :8] = np.random.permutation(np.resize(levels, 8))
        for g in range(8):
            far = levels[np.abs(levels - a[p, g]) >= 10]
            a[p, g + 8] = far[np.random.randint(len(far))]
    return np.exp2(a.ravel()).repeat(32)


def f64(x):
    return np.asarray(x).astype(np.float64)


def striped8(idx):
    return np.asarray(idx).reshape(8, -1, 16).transpose(0, 2, 1).reshape(128, -1).astype(np.uint16)


def unstriped8(offs):
    return offs.reshape(8, 16, -1).transpose(0, 2, 1).reshape(8, -1).astype(np.int64)


def pick8(x, idx, run):
    r = np.arange(len(x))
    return x[r[:, None], idx[r % (8 * run) // run]]


E2M1 = np.array([0.0, 0.5, 1.0, 1.5, 2.0, 3.0, 4.0, 6.0, -0.0, -0.5, -1.0, -1.5, -2.0, -3.0, -4.0, -6.0])


def pack_weight(w, fmt):
    k, n = w.shape
    w = f64(np.asarray(w, np.float32).astype(ml_dtypes.bfloat16)).reshape(k // 32, 32, n)
    amax = np.abs(w).max(1)
    if fmt == "e4m3":
        byte = np.frexp(amax)[1] - 1 + 127 - 7
    else:
        mant, ex = np.frexp(amax / 6.0)
        byte = np.where(mant > 0.5, ex, ex - 1) + 127
    byte = np.clip(np.where(amax > 0, byte, 1), 1, 254)
    scaled = (w * np.exp2(127.0 - byte)[:, None, :]).reshape(k, n).astype(np.float32)
    by_word = np.ascontiguousarray(scaled.reshape(k // 512, 128, 4, n).transpose(0, 1, 3, 2))
    if fmt == "e4m3":
        words = by_word.astype(ml_dtypes.float8_e4m3fn).view(np.uint8)
    else:
        c = by_word.astype(ml_dtypes.float4_e2m1fn).view(np.uint8) & 0xF
        words = (c[..., 0::2] | (c[..., 1::2] << 4)).reshape(k // 512, 128, 2 * n)
    return np.ascontiguousarray(words), np.ascontiguousarray(byte.astype(np.uint8).reshape(k // 512, 16, n))


def unpack_weight(words, scales, fmt):
    g, _, n = scales.shape
    words = np.ascontiguousarray(words).reshape(g, 128, n, -1)
    if fmt == "e4m3":
        vals = words.view(ml_dtypes.float8_e4m3fn).astype(np.float64)
    else:
        nib = np.empty((g, 128, n, 4), np.uint8)
        nib[..., 0::2] = words & 0xF
        nib[..., 1::2] = words >> 4
        vals = E2M1[nib]
    vals = vals * np.repeat(np.exp2(scales.astype(np.float64) - 127.0), 8, axis=1)[..., None]
    return vals.transpose(0, 1, 3, 2).reshape(g * 512, n)


D, E, T, Q, I = 512, 512, 1024, 128, 512


def setup_inputs():
    n = np.random.standard_normal
    idx = np.stack([np.random.permutation(T)[:I] for _ in range(8)])
    idx2 = np.stack([np.random.permutation(T)[:I] for _ in range(8)])
    fd = mx_kscale(D)
    fe = mx_kscale(E)
    keysp = pack_weight(n((D, T)) / fd[:, None], "e4m3")
    return {
        "query": (n((D, Q)) * 0.6 / np.sqrt(D) * fd[:, None]).astype(np.float32),
        "keys_words": keysp[0],
        "keys_scales": keysp[1],
        "gout": (n((E, Q)) * 1 / np.sqrt(E) * fe[:, None]).astype(np.float32),
        "vals": (n((E, T)) / fe[:, None]).astype(np.float32),
        "share": (np.random.uniform(0.4, 0.9, (Q, 1))).astype(np.float32),
        "fac": (np.random.uniform(0.5, 2.0, (1, T))).astype(np.float32),
        "dquery": (n((D, Q)) * 1.0 / np.sqrt(D) * fd[:, None]).astype(np.float32),
        "base": (0.5 * n((Q, T))).astype(np.float32),
        "offs": striped8(idx),
        "offs2": striped8(idx2),
    }


def reference(query, keys_words, keys_scales, gout, vals, share, fac, dquery, base, offs, offs2):
    idx = unstriped8(offs)
    idx2 = unstriped8(offs2)
    keysu = unpack_weight(keys_words, keys_scales, "e4m3")
    queryq = mxq(f64(query), 0, "e4m3")
    a = queryq.T @ keysu
    dqueryq = mxq(f64(dquery), 0, "e4m3")
    ta = dqueryq.T @ keysu
    dl = (pick8(a, idx2, 16) - pick8(a, idx, 16)) * f64(share)
    df0 = np.zeros((Q, T))
    df0[np.arange(Q)[:, None], idx[np.arange(Q) % 128 // 16]] = dl
    s = a + df0
    p = np.exp(s - np.max(s, axis=1, keepdims=True))
    z = np.sum(p, axis=1, keepdims=True)
    goutq = mxq(f64(gout), 0, "e4m3")
    valsq = mxq(f64(vals), 0, "e4m3")
    c0 = goutq.T @ valsq
    dz = np.sum(c0 * p * f64(fac) / np.square(z) * (-1.0), axis=1, keepdims=True)
    dp = c0 / z * f64(fac) + dz
    xdl = (pick8(ta, idx2, 16) - pick8(ta, idx, 16)) * f64(share)
    xdf0 = np.zeros((Q, T))
    xdf0[np.arange(Q)[:, None], idx[np.arange(Q) % 128 // 16]] = xdl
    xs = ta + xdf0
    xp = xs * p
    xz = np.sum(xp, axis=1, keepdims=True)
    xdz = np.sum((xp * f64(fac) * c0 - xz * z * 2.0 * c0 * p * f64(fac) / np.square(z)) / np.square(z) * (-1.0), axis=1, keepdims=True)
    xdp = xz * c0 / np.square(z) * (-1.0) * f64(fac) + xdz
    xds = xdp * p + xp * dp
    xddl = pick8(xds, idx, 16)
    xe1 = xddl * f64(share)
    xs1 = np.zeros((Q, T))
    xs1[np.arange(Q)[:, None], idx2[np.arange(Q) % 128 // 16]] = xe1
    xe2 = xddl * f64(share) * (-1.0)
    xs2 = np.zeros((Q, T))
    xs2[np.arange(Q)[:, None], idx[np.arange(Q) % 128 // 16]] = xe2
    xda = xds + xs1 + xs2
    y = xda * 1024.0 + f64(base)
    return y

@@ -1,0 +1,270 @@
+from contextlib import ExitStack
+
+import concourse.mybir as mybir
+from concourse.masks import make_identity
+
+D, E, T, Q, I = 512, 512, 1024, 128, 512
+FLOPS = 3 * 2 * 512 * Q * T
+
+F32 = mybir.dt.float32
+BF16 = mybir.dt.bfloat16
+I32 = mybir.dt.int32
+U32 = mybir.dt.uint32
+U16 = mybir.dt.uint16
+U8 = mybir.dt.uint8
+FP8X4 = mybir.dt.float8_e4m3fn_x4
+ALU = mybir.AluOpType
+ACT = mybir.ActivationFunctionType
+AXIS_X = mybir.AxisListType.X
+
+P = 128
+PACK = 4
+BANK = 512
+HALVES = T // BANK
+BLOCKS = BANK // P
+OUT_SCALE = 1024.0
+
+
+def tile_attend_hvborrowed_heads_kernel(tc, query, keys_words, keys_scales, gout, vals, share, fac, dquery, base, offs, offs2, out):
+    nc = tc.nc
+
+    def half(h):
+        return slice(h * BANK, (h + 1) * BANK)
+
+    def block(j):
+        return slice(j * P, (j + 1) * P)
+
+    def interleave(copy, grouped, raw):
+        copy(
+            out=grouped.rearrange("p (c i t) -> p c t i", i=4, t=PACK),
+            in_=raw.rearrange("p t (c i) -> p c t i", i=4),
+        )
+
+    with ExitStack() as ctx:
+        sb = ctx.enter_context(tc.tile_pool(name="sb", bufs=1))
+        ps = ctx.enter_context(tc.psum_pool(name="ps", bufs=1))
+
+        def bank(role, h, name):
+            return ps.tile([P, BANK], F32, tag=role + str(h), name=name + str(h))
+
+        k_scales = sb.tile([P, T], U8, align_bytes=64)
+        warm = sb.tile([P, 2], F32)
+        nc.vector.memset(warm[:, 0:1], 0.0)
+        nc.scalar.activation(out=warm[:, 1:2], in_=warm[:, 0:1], func=ACT.Exp)
+        for quad in range(4):
+            nc.scalar.dma_start(
+                out=k_scales[32 * quad : 32 * quad + 4, :].bitcast(I32),
+                in_=keys_scales[0, 4 * quad : 4 * quad + 4, :].bitcast(I32),
+            )
+        q_raw = sb.tile([P, PACK, Q], F32)
+        nc.sync.dma_start(out=q_raw[:], in_=query.rearrange("(p t) q -> p t q", t=PACK))
+        k_words = sb.tile([P, T], U32, align_bytes=64)
+        nc.sync.dma_start(out=k_words[:].bitcast(I32), in_=keys_words[0].rearrange("p n t -> p (n t)").bitcast(I32))
+        dq_raw = sb.tile([P, PACK, Q], F32)
+        nc.sync.dma_start(out=dq_raw[:], in_=dquery.rearrange("(p t) q -> p t q", t=PACK))
+        go_raw = sb.tile([P, PACK, Q], F32)
+        nc.sync.dma_start(out=go_raw[:], in_=gout.rearrange("(p t) q -> p t q", t=PACK))
+        share_col = sb.tile([P, 1], F32)
+        nc.scalar.dma_start(out=share_col[:], in_=share)
+        list1 = sb.tile([P, I // 16], U16)
+        nc.sync.dma_start(list1[:], offs)
+        list2 = sb.tile([P, I // 16], U16)
+        nc.sync.dma_start(list2[:], offs2)
+        v_raw = []
+        for h in range(HALVES):
+            raw = sb.tile([P, PACK, BANK], F32, tag="v_raw%d" % h, name="v_raw%d" % h)
+            nc.sync.dma_start(out=raw[:], in_=vals.rearrange("(p t) n -> p t n", t=PACK)[:, :, half(h)])
+            v_raw.append(raw)
+        base_sb = sb.tile([P, T], F32)
+        nc.sync.dma_start(out=base_sb[:], in_=base)
+
+        fac_rows = sb.tile([P, P], F32)
+        nc.gpsimd.memset(fac_rows[:], 0.0)
+        nc.sync.dma_start(out=fac_rows[0 : T // P, :], in_=fac.rearrange("o (c p) -> (o c) p", p=P))
+        ident = sb.tile([P, P], F32)
+        make_identity(nc, ident[:])
+
+        placed1 = sb.tile([P, T], F32)
+        placed2 = sb.tile([P, T], F32)
+        nc.vector.memset(placed1[:], 0.0)
+        nc.vector.memset(placed2[:], 0.0)
+
+        def add_turned(acc, src, h, first, last):
+            for j in range(BLOCKS):
+                nc.tensor.matmul(
+                    acc[:, block(j)], lhsT=src[:, block(BLOCKS * h + j)], rhs=ident[:], is_transpose=True,
+                    start=(first and j == 0), stop=(last and j == BLOCKS - 1),
+                )
+
+        def turn(dst, src, h):
+            for j in range(BLOCKS):
+                nc.tensor.transpose(dst[:, block(j)], src[:, block(BLOCKS * h + j)], ident[:])
+
+        q_bf = sb.tile([P, Q * PACK], BF16, align_bytes=64, tag="rows_bf")
+        interleave(nc.vector.tensor_copy, q_bf[:], q_raw[:])
+        q_codes = sb.tile([P, Q], U32, align_bytes=64)
+        q_scales = sb.tile([P, Q], U8, align_bytes=64)
+        nc.vector.quantize_mx(out=q_codes[:].bitcast(FP8X4), scales=q_scales[:], in_=q_bf[:])
+
+        a_sb = sb.tile([P, T], F32)
+        for h in range(HALVES):
+            acc = bank("A", h, "a_ps")
+            nc.tensor.matmul_mx(out=acc[:], lhsT=q_codes[:].bitcast(FP8X4), lhsT_scale=q_scales[:],
+                                rhs=k_words[:, half(h)].bitcast(FP8X4), rhs_scale=k_scales[:, half(h)], start=True, stop=True)
+            if h == 0:
+                nc.scalar.copy(out=a_sb[:, half(h)], in_=acc[:])
+            else:
+                nc.vector.tensor_copy(out=a_sb[:, half(h)], in_=acc[:])
+
+        dg_bf = sb.tile([P, 2 * Q * PACK], BF16, align_bytes=64, tag="rows_bf")
+        interleave(nc.vector.tensor_copy, dg_bf[:, 0 : Q * PACK], dq_raw[:])
+        interleave(nc.vector.tensor_copy, dg_bf[:, Q * PACK :], go_raw[:])
+        dg_codes = sb.tile([P, 2 * Q], U32, align_bytes=64)
+        dg_scales = sb.tile([P, 2 * Q], U8, align_bytes=64)
+        nc.vector.quantize_mx(out=dg_codes[:].bitcast(FP8X4), scales=dg_scales[:], in_=dg_bf[:])
+
+        ta_sb = sb.tile([P, T], F32)
+        for h in range(HALVES):
+            acc = bank("B", h, "ta_ps")
+            nc.tensor.matmul_mx(out=acc[:], lhsT=dg_codes[:, 0:Q].bitcast(FP8X4), lhsT_scale=dg_scales[:, 0:Q],
+                                rhs=k_words[:, half(h)].bitcast(FP8X4), rhs_scale=k_scales[:, half(h)], start=True, stop=True)
+            nc.scalar.copy(out=ta_sb[:, half(h)], in_=acc[:])
+
+        share_row = sb.tile([P, I], F32)
+        nc.scalar.activation(out=share_row[:], in_=share_col[:].to_broadcast([P, I]), func=ACT.Copy)
+
+        fac_ps = bank("B", 0, "fac_ps")
+        nc.tensor.transpose(fac_ps[:, 0:P], fac_rows[:], ident[:])
+        fac_cols = sb.tile([P, T // P], F32)
+        nc.scalar.copy(out=fac_cols[:], in_=fac_ps[:, 0 : T // P])
+
+        a_at1 = sb.tile([P, I], F32)
+        a_diff = sb.tile([P, I], F32)
+        nc.vector.tensor_copy(a_at1[:], a_sb[:].indirect(list1[:]))
+        nc.vector.tensor_tensor(a_diff[:], a_sb[:].indirect(list2[:]), a_at1[:], ALU.subtract)
+        nc.vector.tensor_tensor(placed1[:].indirect(list1[:]), a_diff[:], share_row[:], ALU.mult)
+
+        v_bf = []
+        for h in range(HALVES):
+            grouped = sb.tile([P, BANK * PACK], BF16, align_bytes=64, name="v_bf%d" % h)
+            interleave(nc.scalar.copy, grouped[:], v_raw[h][:])
+            v_bf.append(grouped)
+
+        sT_ps = [bank("C", h, "sT_ps") for h in range(HALVES)]
+        for h in range(HALVES):
+            add_turned(sT_ps[h], a_sb, h, True, False)
+        sT_sb = sb.tile([P, T], F32, tag="v_raw1")
+        for h in range(HALVES):
+            add_turned(sT_ps[h], placed1, h, False, True)
+            nc.scalar.copy(out=sT_sb[:, half(h)], in_=sT_ps[h][:])
+        s_ps = [bank("A", h, "s_ps") for h in range(HALVES)]
+        for h in range(HALVES):
+            turn(s_ps[h], sT_sb, h)
+
+        ta_at1 = sb.tile([P, I], F32)
+        ta_diff = sb.tile([P, I], F32)
+        cut = I // 2
+        nc.vector.tensor_copy(ta_at1[:], ta_sb[:].indirect(list1[:]))
+        nc.vector.tensor_tensor(ta_diff[:, 0:cut], ta_sb[:].indirect(list2[:, 0 : cut // 16]), ta_at1[:, 0:cut], ALU.subtract)
+
+        v_codes = sb.tile([P, T], U32, align_bytes=64)
+        v_scales = sb.tile([P, T], U8, align_bytes=64)
+        gT_sb = sb.tile([P, T], F32)
+        g_ps = []
+        for h in range(HALVES):
+            nc.vector.quantize_mx(out=v_codes[:, half(h)].bitcast(FP8X4), scales=v_scales[:, half(h)], in_=v_bf[h][:])
+            acc = bank("C", 1 - h, "c0T_ps")
+            for j in range(BLOCKS):
+                cols = block(BLOCKS * h + j)
+                nc.tensor.matmul_mx(out=acc[:, block(j)], lhsT=v_codes[:, cols].bitcast(FP8X4), lhsT_scale=v_scales[:, cols],
+                                    rhs=dg_codes[:, Q:].bitcast(FP8X4), rhs_scale=dg_scales[:, Q:], start=True, stop=True)
+            for j in range(BLOCKS):
+                c = BLOCKS * h + j
+                nc.scalar.activation(out=gT_sb[:, block(c)], in_=acc[:, block(j)], func=ACT.Copy, scale=fac_cols[:, c : c + 1])
+            g_h = bank("C", 1 - h, "g_ps")
+            turn(g_h, gT_sb, h)
+            g_ps.append(g_h)
+
+        half_max = ta_diff[:, cut : cut + HALVES]
+        for h in range(HALVES):
+            nc.vector.tensor_reduce(out=half_max[:, h : h + 1], in_=s_ps[h][:], axis=AXIS_X, op=ALU.max)
+        neg_max = sb.tile([P, 1], F32)
+        nc.vector.tensor_reduce(out=neg_max[:], in_=half_max, axis=AXIS_X, op=ALU.max, negate=True)
+        p = sb.tile([P, T], F32)
+        z_halves = sb.tile([P, HALVES], F32)
+        for h in range(HALVES):
+            nc.scalar.activation(out=p[:, half(h)], in_=s_ps[h][:], func=ACT.Exp, bias=neg_max[:], accum_out=z_halves[:, h : h + 1])
+        z_scaled_halves = sb.tile([P, HALVES], F32)
+        z_scaled = sb.tile([P, 1], F32)
+        nc.scalar.activation(out=z_scaled_halves[:], in_=z_halves[:], func=ACT.Copy, scale=1.0 / OUT_SCALE, accum_out=z_scaled[:])
+
+        xsT_ps = [bank("A", h, "xsT_ps") for h in range(HALVES)]
+        for h in range(HALVES):
+            add_turned(xsT_ps[h], ta_sb, h, True, False)
+        nc.vector.tensor_tensor(ta_diff[:, cut:], ta_sb[:].indirect(list2[:, cut // 16 :]), ta_at1[:, cut:], ALU.subtract)
+        nc.vector.tensor_tensor(placed1[:].indirect(list1[:]), ta_diff[:], share_row[:], ALU.mult)
+        xsT_sb = sb.tile([P, T], F32)
+        for h in range(HALVES):
+            add_turned(xsT_ps[h], placed1, h, False, True)
+            nc.scalar.copy(out=xsT_sb[:, half(h)], in_=xsT_ps[h][:])
+        xs_ps = [bank("B", h, "xs_ps") for h in range(HALVES)]
+        for h in range(HALVES):
+            turn(xs_ps[h], xsT_sb, h)
+
+        neg_share_row = sb.tile([P, I], F32)
+        nc.scalar.activation(out=neg_share_row[:], in_=share_col[:].to_broadcast([P, I]), func=ACT.Copy, scale=-1.0)
+
+        k = sb.tile([P, 1], F32)
+        nc.vector.reciprocal(out=k[:], in_=z_scaled[:])
+        neg_r = sb.tile([P, 1], F32)
+        nc.vector.tensor_scalar(out=neg_r[:], in0=k[:], scalar1=-1.0 / OUT_SCALE, scalar2=None, op0=ALU.mult)
+
+        gp = sb.tile([P, T], F32)
+        gp_sums = sb.tile([P, HALVES], F32)
+        for h in range(HALVES):
+            nc.vector.scalar_tensor_tensor(out=gp[:, half(h)], in0=g_ps[h][:], scalar=k[:], in1=p[:, half(h)],
+                                           op0=ALU.mult, op1=ALU.mult, accum_out=gp_sums[:, h : h + 1])
+        neg_g_mean = sb.tile([P, 1], F32)
+        nc.vector.tensor_scalar(out=neg_g_mean[:], in0=gp_sums[:, 0:1], scalar1=gp_sums[:, 1:2], scalar2=neg_r[:], op0=ALU.add, op1=ALU.mult)
+        centred = sb.tile([P, T], F32)
+        nc.vector.scalar_tensor_tensor(out=centred[:, half(0)], in0=p[:, half(0)], scalar=neg_g_mean[:], in1=gp[:, half(0)], op0=ALU.mult, op1=ALU.add)
+
+        xp = sb.tile([P, T], F32)
+        xp_sums = sb.tile([P, HALVES], F32)
+        for h in range(HALVES):
+            nc.vector.scalar_tensor_tensor(out=xp[:, half(h)], in0=xs_ps[h][:], scalar=neg_r[:], in1=p[:, half(h)],
+                                           op0=ALU.mult, op1=ALU.mult, accum_out=xp_sums[:, h : h + 1])
+        neg_xs_mean = sb.tile([P, 1], F32)
+        nc.vector.tensor_tensor(out=neg_xs_mean[:], in0=xp_sums[:, 0:1], in1=xp_sums[:, 1:2], op=ALU.add)
+
+        nc.vector.scalar_tensor_tensor(out=centred[:, half(1)], in0=p[:, half(1)], scalar=neg_g_mean[:], in1=gp[:, half(1)], op0=ALU.mult, op1=ALU.add)
+        both = sb.tile([P, T], F32)
+        both_sums = sb.tile([P, HALVES], F32)
+        for h in range(HALVES):
+            nc.vector.scalar_tensor_tensor(out=both[:, half(h)], in0=xs_ps[h][:], scalar=neg_xs_mean[:], in1=centred[:, half(h)],
+                                           op0=ALU.add, op1=ALU.mult, accum_out=both_sums[:, h : h + 1])
+        neg_cov = sb.tile([P, 1], F32)
+        nc.vector.tensor_scalar(out=neg_cov[:], in0=both_sums[:, 0:1], scalar1=both_sums[:, 1:2], scalar2=neg_r[:], op0=ALU.add, op1=ALU.mult)
+        xds = sb.tile([P, T], F32)
+        nc.vector.scalar_tensor_tensor(out=xds[:], in0=p[:], scalar=neg_cov[:], in1=both[:], op0=ALU.mult, op1=ALU.add)
+
+        uT_ps = [bank("D", h, "uT_ps") for h in range(HALVES)]
+        for h in range(HALVES):
+            add_turned(uT_ps[h], base_sb, h, True, False)
+        xddl = sb.tile([P, I], F32)
+        nc.vector.tensor_copy(xddl[:], xds[:].indirect(list1[:]))
+        for h in range(HALVES):
+            add_turned(uT_ps[h], xds, h, False, False)
+        nc.vector.tensor_tensor(placed1[:].indirect(list1[:]), xddl[:], neg_share_row[:], ALU.mult)
+        uT_sb = sb.tile([P, T], F32)
+        for h in range(HALVES):
+            add_turned(uT_ps[h], placed1, h, False, True)
+            nc.scalar.copy(out=uT_sb[:, half(h)], in_=uT_ps[h][:])
+        u_ps = [bank("C", h, "u_ps") for h in range(HALVES)]
+        for h in range(HALVES):
+            turn(u_ps[h], uT_sb, h)
+        nc.vector.tensor_tensor(placed2[:].indirect(list2[:]), xddl[:], share_row[:], ALU.mult)
+        result = sb.tile([P, T], F32)
+        for h in range(HALVES):
+            nc.vector.tensor_tensor(out=result[:, half(h)], in0=u_ps[h][:], in1=placed2[:, half(h)], op=ALU.add)
+            (nc.sync if h == 0 else nc.scalar).dma_start(out=out[:, half(h)], in_=result[:, half(h)])

@@ -22,6 +22,7 @@ PACK = 4
 BANK = 512
 HALVES = T // BANK
 BLOCKS = BANK // P
+QUARTER = T // 4
 OUT_SCALE = 1024.0
 
 
@@ -30,6 +31,15 @@ def tile_attend_hvborrowed_heads_kernel(tc, query, keys_words, keys_scales, gout
 
     def half(h):
         return slice(h * BANK, (h + 1) * BANK)
+
+    def quarter(c):
+        return slice(c * QUARTER, (c + 1) * QUARTER)
+
+    def slots(s):
+        return slice(s * I // 2, (s + 1) * I // 2)
+
+    def entries(s):
+        return slice(s * I // 32, (s + 1) * I // 32)
 
     def block(j):
         return slice(j * P, (j + 1) * P)
@@ -64,8 +74,6 @@ def tile_attend_hvborrowed_heads_kernel(tc, query, keys_words, keys_scales, gout
         nc.sync.dma_start(out=dq_raw[:], in_=dquery.rearrange("(p t) q -> p t q", t=PACK))
         go_raw = sb.tile([P, PACK, Q], F32)
         nc.sync.dma_start(out=go_raw[:], in_=gout.rearrange("(p t) q -> p t q", t=PACK))
-        share_col = sb.tile([P, 1], F32)
-        nc.scalar.dma_start(out=share_col[:], in_=share)
         list1 = sb.tile([P, I // 16], U16)
         nc.sync.dma_start(list1[:], offs)
         list2 = sb.tile([P, I // 16], U16)
@@ -83,18 +91,23 @@ def tile_attend_hvborrowed_heads_kernel(tc, query, keys_words, keys_scales, gout
         nc.sync.dma_start(out=fac_rows[0 : T // P, :], in_=fac.rearrange("o (c p) -> (o c) p", p=P))
         ident = sb.tile([P, P], F32)
         make_identity(nc, ident[:])
+        share_col = sb.tile([P, 1], F32)
+        nc.gpsimd.dma_start(out=share_col[:], in_=share)
 
         placed1 = sb.tile([P, T], F32)
         placed2 = sb.tile([P, T], F32)
         nc.vector.memset(placed1[:], 0.0)
         nc.vector.memset(placed2[:], 0.0)
 
-        def add_turned(acc, src, h, first, last):
-            for j in range(BLOCKS):
+        def add_turned(acc, src, c, first, last):
+            for j in range(2):
                 nc.tensor.matmul(
-                    acc[:, block(j)], lhsT=src[:, block(BLOCKS * h + j)], rhs=ident[:], is_transpose=True,
-                    start=(first and j == 0), stop=(last and j == BLOCKS - 1),
+                    acc[:, block(j)], lhsT=src[:, block(2 * c + j)], rhs=ident[:], is_transpose=True,
+                    start=(first and j == 0), stop=(last and j == 1),
                 )
+
+        def four_banks(roles, name):
+            return [bank(roles[c // 2], c % 2, name + str(c // 2)) for c in range(4)]
 
         def turn(dst, src, h):
             for j in range(BLOCKS):
@@ -107,14 +120,15 @@ def tile_attend_hvborrowed_heads_kernel(tc, query, keys_words, keys_scales, gout
         nc.vector.quantize_mx(out=q_codes[:].bitcast(FP8X4), scales=q_scales[:], in_=q_bf[:])
 
         a_sb = sb.tile([P, T], F32)
-        for h in range(HALVES):
-            acc = bank("A", h, "a_ps")
-            nc.tensor.matmul_mx(out=acc[:], lhsT=q_codes[:].bitcast(FP8X4), lhsT_scale=q_scales[:],
-                                rhs=k_words[:, half(h)].bitcast(FP8X4), rhs_scale=k_scales[:, half(h)], start=True, stop=True)
-            if h == 0:
-                nc.scalar.copy(out=a_sb[:, half(h)], in_=acc[:])
+        for c in range(4):
+            acc = bank("AD"[c // 2], c % 2, "a_ps" + str(c // 2))
+            cols = quarter(c)
+            nc.tensor.matmul_mx(out=acc[:, 0:QUARTER], lhsT=q_codes[:].bitcast(FP8X4), lhsT_scale=q_scales[:],
+                                rhs=k_words[:, cols].bitcast(FP8X4), rhs_scale=k_scales[:, cols], start=True, stop=True)
+            if c < 3:
+                nc.scalar.copy(out=a_sb[:, cols], in_=acc[:, 0:QUARTER])
             else:
-                nc.vector.tensor_copy(out=a_sb[:, half(h)], in_=acc[:])
+                nc.vector.tensor_copy(out=a_sb[:, cols], in_=acc[:, 0:QUARTER])
 
         dg_bf = sb.tile([P, 2 * Q * PACK], BF16, align_bytes=64, tag="rows_bf")
         interleave(nc.vector.tensor_copy, dg_bf[:, 0 : Q * PACK], dq_raw[:])
@@ -138,10 +152,12 @@ def tile_attend_hvborrowed_heads_kernel(tc, query, keys_words, keys_scales, gout
         fac_cols = sb.tile([P, T // P], F32)
         nc.scalar.copy(out=fac_cols[:], in_=fac_ps[:, 0 : T // P])
 
-        a_at1 = sb.tile([P, I], F32)
+        a_at1 = sb.tile([P, I], F32, tag="at1")
         a_diff = sb.tile([P, I], F32)
-        nc.vector.tensor_copy(a_at1[:], a_sb[:].indirect(list1[:]))
-        nc.vector.tensor_tensor(a_diff[:], a_sb[:].indirect(list2[:]), a_at1[:], ALU.subtract)
+        for s in range(2):
+            nc.vector.tensor_copy(a_at1[:, slots(s)], a_sb[:].indirect(list1[:, entries(s)]))
+        for s in range(2):
+            nc.vector.tensor_tensor(a_diff[:, slots(s)], a_sb[:].indirect(list2[:, entries(s)]), a_at1[:, slots(s)], ALU.subtract)
         nc.vector.tensor_tensor(placed1[:].indirect(list1[:]), a_diff[:], share_row[:], ALU.mult)
 
         v_bf = []
@@ -150,22 +166,23 @@ def tile_attend_hvborrowed_heads_kernel(tc, query, keys_words, keys_scales, gout
             interleave(nc.scalar.copy, grouped[:], v_raw[h][:])
             v_bf.append(grouped)
 
-        sT_ps = [bank("C", h, "sT_ps") for h in range(HALVES)]
-        for h in range(HALVES):
-            add_turned(sT_ps[h], a_sb, h, True, False)
+        sT_ps = four_banks("CD", "sT_ps")
+        for c in range(4):
+            add_turned(sT_ps[c], a_sb, c, True, False)
         sT_sb = sb.tile([P, T], F32, tag="v_raw1")
-        for h in range(HALVES):
-            add_turned(sT_ps[h], placed1, h, False, True)
-            nc.scalar.copy(out=sT_sb[:, half(h)], in_=sT_ps[h][:])
+        for c in range(4):
+            add_turned(sT_ps[c], placed1, c, False, True)
+            nc.scalar.copy(out=sT_sb[:, quarter(c)], in_=sT_ps[c][:, 0:QUARTER])
         s_ps = [bank("A", h, "s_ps") for h in range(HALVES)]
         for h in range(HALVES):
             turn(s_ps[h], sT_sb, h)
 
-        ta_at1 = sb.tile([P, I], F32)
-        ta_diff = sb.tile([P, I], F32)
-        cut = I // 2
-        nc.vector.tensor_copy(ta_at1[:], ta_sb[:].indirect(list1[:]))
-        nc.vector.tensor_tensor(ta_diff[:, 0:cut], ta_sb[:].indirect(list2[:, 0 : cut // 16]), ta_at1[:, 0:cut], ALU.subtract)
+        ta_at1 = sb.tile([P, I], F32, tag="at1")
+        ta_room = sb.tile([P, I // 2 + BANK], F32)
+        ta_diff = ta_room[:, 0:I]
+        for s in range(2):
+            nc.vector.tensor_copy(ta_at1[:, slots(s)], ta_sb[:].indirect(list1[:, entries(s)]))
+        nc.vector.tensor_tensor(ta_diff[:, slots(0)], ta_sb[:].indirect(list2[:, entries(0)]), ta_at1[:, slots(0)], ALU.subtract)
 
         v_codes = sb.tile([P, T], U32, align_bytes=64)
         v_scales = sb.tile([P, T], U8, align_bytes=64)
@@ -173,7 +190,7 @@ def tile_attend_hvborrowed_heads_kernel(tc, query, keys_words, keys_scales, gout
         g_ps = []
         for h in range(HALVES):
             nc.vector.quantize_mx(out=v_codes[:, half(h)].bitcast(FP8X4), scales=v_scales[:, half(h)], in_=v_bf[h][:])
-            acc = bank("C", 1 - h, "c0T_ps")
+            acc = bank("D", 1 - h, "c0T_ps")
             for j in range(BLOCKS):
                 cols = block(BLOCKS * h + j)
                 nc.tensor.matmul_mx(out=acc[:, block(j)], lhsT=v_codes[:, cols].bitcast(FP8X4), lhsT_scale=v_scales[:, cols],
@@ -181,90 +198,81 @@ def tile_attend_hvborrowed_heads_kernel(tc, query, keys_words, keys_scales, gout
             for j in range(BLOCKS):
                 c = BLOCKS * h + j
                 nc.scalar.activation(out=gT_sb[:, block(c)], in_=acc[:, block(j)], func=ACT.Copy, scale=fac_cols[:, c : c + 1])
-            g_h = bank("C", 1 - h, "g_ps")
+            g_h = bank("D", 1 - h, "g_ps")
             turn(g_h, gT_sb, h)
             g_ps.append(g_h)
 
-        half_max = ta_diff[:, cut : cut + HALVES]
-        for h in range(HALVES):
-            nc.vector.tensor_reduce(out=half_max[:, h : h + 1], in_=s_ps[h][:], axis=AXIS_X, op=ALU.max)
+        neg_s1 = sb.tile([P, BANK], F32)
+        neg_max_half = sb.tile([P, 1], F32)
         neg_max = sb.tile([P, 1], F32)
-        nc.vector.tensor_reduce(out=neg_max[:], in_=half_max, axis=AXIS_X, op=ALU.max, negate=True)
+        nc.vector.tensor_scalar(out=ta_room[:, I // 2 :], in0=s_ps[0][:], scalar1=-1.0, scalar2=None,
+                                op0=ALU.mult, op1=ALU.min, accum_out=neg_max_half[:])
+        nc.vector.tensor_tensor(ta_diff[:, slots(1)], ta_sb[:].indirect(list2[:, entries(1)]), ta_at1[:, slots(1)], ALU.subtract)
+        nc.vector.tensor_scalar(out=neg_s1[:], in0=s_ps[1][:], scalar1=-1.0, scalar2=neg_max_half[:],
+                                op0=ALU.mult, op1=ALU.min, accum_out=neg_max[:])
         p = sb.tile([P, T], F32)
         z_halves = sb.tile([P, HALVES], F32)
         for h in range(HALVES):
             nc.scalar.activation(out=p[:, half(h)], in_=s_ps[h][:], func=ACT.Exp, bias=neg_max[:], accum_out=z_halves[:, h : h + 1])
-        z_scaled_halves = sb.tile([P, HALVES], F32)
-        z_scaled = sb.tile([P, 1], F32)
-        nc.scalar.activation(out=z_scaled_halves[:], in_=z_halves[:], func=ACT.Copy, scale=1.0 / OUT_SCALE, accum_out=z_scaled[:])
+        z = sb.tile([P, 2], F32)
+        z_parts = sb.tile([P, 2, HALVES], F32)
+        for c, scale in enumerate((1.0, -1.0 / OUT_SCALE)):
+            nc.scalar.activation(out=z_parts[:, c, :], in_=z_halves[:], func=ACT.Copy, scale=scale, accum_out=z[:, c : c + 1])
 
-        xsT_ps = [bank("A", h, "xsT_ps") for h in range(HALVES)]
+        nc.vector.tensor_tensor(placed1[:].indirect(list1[:]), ta_diff, share_row[:], ALU.mult)
+        xs = sb.tile([P, T], F32)
         for h in range(HALVES):
-            add_turned(xsT_ps[h], ta_sb, h, True, False)
-        nc.vector.tensor_tensor(ta_diff[:, cut:], ta_sb[:].indirect(list2[:, cut // 16 :]), ta_at1[:, cut:], ALU.subtract)
-        nc.vector.tensor_tensor(placed1[:].indirect(list1[:]), ta_diff[:], share_row[:], ALU.mult)
-        xsT_sb = sb.tile([P, T], F32)
-        for h in range(HALVES):
-            add_turned(xsT_ps[h], placed1, h, False, True)
-            nc.scalar.copy(out=xsT_sb[:, half(h)], in_=xsT_ps[h][:])
-        xs_ps = [bank("B", h, "xs_ps") for h in range(HALVES)]
-        for h in range(HALVES):
-            turn(xs_ps[h], xsT_sb, h)
+            nc.gpsimd.tensor_tensor(out=xs[:, half(h)], in0=ta_sb[:, half(h)], in1=placed1[:, half(h)], op=ALU.add)
 
+        inv = sb.tile([P, 2], F32)
+        nc.vector.reciprocal(out=inv[:], in_=z[:])
+        r, neg_k = inv[:, 0:1], inv[:, 1:2]
+        pk_room = sb.tile([P, BANK + T], F32)
+        neg_pk = pk_room[:, BANK:]
+        for h in range(HALVES):
+            nc.scalar.activation(out=neg_pk[:, half(h)], in_=p[:, half(h)], func=ACT.Copy, scale=neg_k)
+        prob = sb.tile([P, T], F32)
+        nc.scalar.activation(out=prob[:], in_=p[:], func=ACT.Copy, scale=r)
         neg_share_row = sb.tile([P, I], F32)
         nc.scalar.activation(out=neg_share_row[:], in_=share_col[:].to_broadcast([P, I]), func=ACT.Copy, scale=-1.0)
 
-        k = sb.tile([P, 1], F32)
-        nc.vector.reciprocal(out=k[:], in_=z_scaled[:])
-        neg_r = sb.tile([P, 1], F32)
-        nc.vector.tensor_scalar(out=neg_r[:], in0=k[:], scalar1=-1.0 / OUT_SCALE, scalar2=None, op0=ALU.mult)
-
         gp = sb.tile([P, T], F32)
-        gp_sums = sb.tile([P, HALVES], F32)
+        g_mean_halves = sb.tile([P, HALVES], F32)
         for h in range(HALVES):
-            nc.vector.scalar_tensor_tensor(out=gp[:, half(h)], in0=g_ps[h][:], scalar=k[:], in1=p[:, half(h)],
-                                           op0=ALU.mult, op1=ALU.mult, accum_out=gp_sums[:, h : h + 1])
-        neg_g_mean = sb.tile([P, 1], F32)
-        nc.vector.tensor_scalar(out=neg_g_mean[:], in0=gp_sums[:, 0:1], scalar1=gp_sums[:, 1:2], scalar2=neg_r[:], op0=ALU.add, op1=ALU.mult)
+            nc.vector.scalar_tensor_tensor(out=gp[:, half(h)], in0=g_ps[h][:], scalar=1.0, in1=p[:, half(h)],
+                                           op0=ALU.mult, op1=ALU.mult, accum_out=g_mean_halves[:, h : h + 1])
+        g_mean = sb.tile([P, 1], F32)
+        nc.vector.tensor_scalar(out=g_mean[:], in0=g_mean_halves[:, 0:1], scalar1=g_mean_halves[:, 1:2], scalar2=r, op0=ALU.add, op1=ALU.mult)
         centred = sb.tile([P, T], F32)
-        nc.vector.scalar_tensor_tensor(out=centred[:, half(0)], in0=p[:, half(0)], scalar=neg_g_mean[:], in1=gp[:, half(0)], op0=ALU.mult, op1=ALU.add)
-
-        xp = sb.tile([P, T], F32)
-        xp_sums = sb.tile([P, HALVES], F32)
         for h in range(HALVES):
-            nc.vector.scalar_tensor_tensor(out=xp[:, half(h)], in0=xs_ps[h][:], scalar=neg_r[:], in1=p[:, half(h)],
-                                           op0=ALU.mult, op1=ALU.mult, accum_out=xp_sums[:, h : h + 1])
-        neg_xs_mean = sb.tile([P, 1], F32)
-        nc.vector.tensor_tensor(out=neg_xs_mean[:], in0=xp_sums[:, 0:1], in1=xp_sums[:, 1:2], op=ALU.add)
-
-        nc.vector.scalar_tensor_tensor(out=centred[:, half(1)], in0=p[:, half(1)], scalar=neg_g_mean[:], in1=gp[:, half(1)], op0=ALU.mult, op1=ALU.add)
+            nc.vector.scalar_tensor_tensor(out=centred[:, half(h)], in0=g_ps[h][:], scalar=g_mean[:], in1=neg_pk[:, half(h)],
+                                           op0=ALU.subtract, op1=ALU.mult)
+        xs_mean = sb.tile([P, 1], F32)
+        nc.vector.scalar_tensor_tensor(out=pk_room[:, 0:T], in0=xs[:], scalar=r, in1=p[:], op0=ALU.mult, op1=ALU.mult, accum_out=xs_mean[:])
         both = sb.tile([P, T], F32)
-        both_sums = sb.tile([P, HALVES], F32)
-        for h in range(HALVES):
-            nc.vector.scalar_tensor_tensor(out=both[:, half(h)], in0=xs_ps[h][:], scalar=neg_xs_mean[:], in1=centred[:, half(h)],
-                                           op0=ALU.add, op1=ALU.mult, accum_out=both_sums[:, h : h + 1])
-        neg_cov = sb.tile([P, 1], F32)
-        nc.vector.tensor_scalar(out=neg_cov[:], in0=both_sums[:, 0:1], scalar1=both_sums[:, 1:2], scalar2=neg_r[:], op0=ALU.add, op1=ALU.mult)
+        both_sum = sb.tile([P, 1], F32)
+        nc.vector.scalar_tensor_tensor(out=both[:], in0=xs[:], scalar=xs_mean[:], in1=centred[:],
+                                       op0=ALU.subtract, op1=ALU.mult, accum_out=both_sum[:])
         xds = sb.tile([P, T], F32)
-        nc.vector.scalar_tensor_tensor(out=xds[:], in0=p[:], scalar=neg_cov[:], in1=both[:], op0=ALU.mult, op1=ALU.add)
+        nc.vector.scalar_tensor_tensor(out=xds[:], in0=prob[:], scalar=both_sum[:], in1=both[:], op0=ALU.mult, op1=ALU.subtract)
 
-        uT_ps = [bank("D", h, "uT_ps") for h in range(HALVES)]
-        for h in range(HALVES):
-            add_turned(uT_ps[h], base_sb, h, True, False)
+        uT_ps = four_banks("BA", "uT_ps")
+        for c in range(4):
+            add_turned(uT_ps[c], base_sb, c, True, False)
         xddl = sb.tile([P, I], F32)
         nc.vector.tensor_copy(xddl[:], xds[:].indirect(list1[:]))
-        for h in range(HALVES):
-            add_turned(uT_ps[h], xds, h, False, False)
+        for c in range(4):
+            add_turned(uT_ps[c], xds, c, False, False)
         nc.vector.tensor_tensor(placed1[:].indirect(list1[:]), xddl[:], neg_share_row[:], ALU.mult)
         uT_sb = sb.tile([P, T], F32)
-        for h in range(HALVES):
-            add_turned(uT_ps[h], placed1, h, False, True)
-            nc.scalar.copy(out=uT_sb[:, half(h)], in_=uT_ps[h][:])
+        for c in range(4):
+            add_turned(uT_ps[c], placed1, c, False, True)
+            nc.scalar.copy(out=uT_sb[:, quarter(c)], in_=uT_ps[c][:, 0:QUARTER])
         u_ps = [bank("C", h, "u_ps") for h in range(HALVES)]
         for h in range(HALVES):
             turn(u_ps[h], uT_sb, h)
         nc.vector.tensor_tensor(placed2[:].indirect(list2[:]), xddl[:], share_row[:], ALU.mult)
         result = sb.tile([P, T], F32)
-        for h in range(HALVES):
-            nc.vector.tensor_tensor(out=result[:, half(h)], in0=u_ps[h][:], in1=placed2[:, half(h)], op=ALU.add)
-            (nc.sync if h == 0 else nc.scalar).dma_start(out=out[:, half(h)], in_=result[:, half(h)])
+        for c in range(4):
+            nc.vector.tensor_tensor(out=result[:, quarter(c)], in0=u_ps[c // 2][:, quarter(c % 2)], in1=placed2[:, quarter(c)], op=ALU.add)
+            (nc.sync if c % 2 == 0 else nc.scalar).dma_start(out=out[:, quarter(c)], in_=result[:, quarter(c)])

@@ -23,6 +23,7 @@ BANK = 512
 HALVES = T // BANK
 BLOCKS = BANK // P
 QUARTER = T // 4
+Q_SPLIT = 80
 OUT_SCALE = 1024.0
 
 
@@ -114,7 +115,8 @@ def tile_attend_hvborrowed_heads_kernel(tc, query, keys_words, keys_scales, gout
                 nc.tensor.transpose(dst[:, block(j)], src[:, block(BLOCKS * h + j)], ident[:])
 
         q_bf = sb.tile([P, Q * PACK], BF16, align_bytes=64, tag="rows_bf")
-        interleave(nc.vector.tensor_copy, q_bf[:], q_raw[:])
+        interleave(nc.vector.tensor_copy, q_bf[:, 0 : Q_SPLIT * PACK], q_raw[:, :, 0:Q_SPLIT])
+        interleave(nc.scalar.copy, q_bf[:, Q_SPLIT * PACK :], q_raw[:, :, Q_SPLIT:])
         q_codes = sb.tile([P, Q], U32, align_bytes=64)
         q_scales = sb.tile([P, Q], U8, align_bytes=64)
         nc.vector.quantize_mx(out=q_codes[:].bitcast(FP8X4), scales=q_scales[:], in_=q_bf[:])
@@ -233,8 +235,6 @@ def tile_attend_hvborrowed_heads_kernel(tc, query, keys_words, keys_scales, gout
             nc.scalar.activation(out=neg_pk[:, half(h)], in_=p[:, half(h)], func=ACT.Copy, scale=neg_k)
         prob = sb.tile([P, T], F32)
         nc.scalar.activation(out=prob[:], in_=p[:], func=ACT.Copy, scale=r)
-        neg_share_row = sb.tile([P, I], F32)
-        nc.scalar.activation(out=neg_share_row[:], in_=share_col[:].to_broadcast([P, I]), func=ACT.Copy, scale=-1.0)
 
         gp = sb.tile([P, T], F32)
         g_mean_halves = sb.tile([P, HALVES], F32)
@@ -242,7 +242,8 @@ def tile_attend_hvborrowed_heads_kernel(tc, query, keys_words, keys_scales, gout
             nc.vector.scalar_tensor_tensor(out=gp[:, half(h)], in0=g_ps[h][:], scalar=1.0, in1=p[:, half(h)],
                                            op0=ALU.mult, op1=ALU.mult, accum_out=g_mean_halves[:, h : h + 1])
         g_mean = sb.tile([P, 1], F32)
-        nc.vector.tensor_scalar(out=g_mean[:], in0=g_mean_halves[:, 0:1], scalar1=g_mean_halves[:, 1:2], scalar2=r, op0=ALU.add, op1=ALU.mult)
+        g_mean_parts = sb.tile([P, HALVES], F32)
+        nc.vector.tensor_scalar(out=g_mean_parts[:], in0=g_mean_halves[:], scalar1=r, scalar2=None, op0=ALU.mult, op1=ALU.add, accum_out=g_mean[:])
         centred = sb.tile([P, T], F32)
         for h in range(HALVES):
             nc.vector.scalar_tensor_tensor(out=centred[:, half(h)], in0=g_ps[h][:], scalar=g_mean[:], in1=neg_pk[:, half(h)],
@@ -259,20 +260,22 @@ def tile_attend_hvborrowed_heads_kernel(tc, query, keys_words, keys_scales, gout
         uT_ps = four_banks("BA", "uT_ps")
         for c in range(4):
             add_turned(uT_ps[c], base_sb, c, True, False)
-        xddl = sb.tile([P, I], F32)
-        nc.vector.tensor_copy(xddl[:], xds[:].indirect(list1[:]))
+        xe1 = sb.tile([P, I], F32)
+        nc.vector.tensor_tensor(xe1[:], xds[:].indirect(list1[:]), share_row[:], ALU.mult)
         for c in range(4):
             add_turned(uT_ps[c], xds, c, False, False)
-        nc.vector.tensor_tensor(placed1[:].indirect(list1[:]), xddl[:], neg_share_row[:], ALU.mult)
+        nc.vector.tensor_copy(placed2[:].indirect(list2[:]), xe1[:])
+        xe2 = sb.tile([P, I], F32)
+        nc.scalar.activation(out=xe2[:], in_=xe1[:], func=ACT.Copy, scale=-1.0)
         uT_sb = sb.tile([P, T], F32)
         for c in range(4):
-            add_turned(uT_ps[c], placed1, c, False, True)
+            add_turned(uT_ps[c], placed2, c, False, True)
             nc.scalar.copy(out=uT_sb[:, quarter(c)], in_=uT_ps[c][:, 0:QUARTER])
         u_ps = [bank("C", h, "u_ps") for h in range(HALVES)]
         for h in range(HALVES):
             turn(u_ps[h], uT_sb, h)
-        nc.vector.tensor_tensor(placed2[:].indirect(list2[:]), xddl[:], share_row[:], ALU.mult)
+        nc.vector.tensor_copy(placed1[:].indirect(list1[:]), xe2[:])
         result = sb.tile([P, T], F32)
         for c in range(4):
-            nc.vector.tensor_tensor(out=result[:, quarter(c)], in0=u_ps[c // 2][:, quarter(c % 2)], in1=placed2[:, quarter(c)], op=ALU.add)
+            nc.vector.tensor_tensor(out=result[:, quarter(c)], in0=u_ps[c // 2][:, quarter(c % 2)], in1=placed1[:, quarter(c)], op=ALU.add)
             (nc.sync if c % 2 == 0 else nc.scalar).dma_start(out=out[:, quarter(c)], in_=result[:, quarter(c)])

@@ -24,6 +24,7 @@ HALVES = T // BANK
 BLOCKS = BANK // P
 QUARTER = T // 4
 Q_SPLIT = 80
+VAL_LOADS = ((0, 256), (256, 512), (512, 1024))
 OUT_SCALE = 1024.0
 
 
@@ -62,28 +63,28 @@ def tile_attend_hvborrowed_heads_kernel(tc, query, keys_words, keys_scales, gout
         warm = sb.tile([P, 2], F32)
         nc.vector.memset(warm[:, 0:1], 0.0)
         nc.scalar.activation(out=warm[:, 1:2], in_=warm[:, 0:1], func=ACT.Exp)
+        q_raw = sb.tile([P, PACK, Q], F32)
+        nc.sync.dma_start(out=q_raw[:], in_=query.rearrange("(p t) q -> p t q", t=PACK))
         for quad in range(4):
-            nc.scalar.dma_start(
+            nc.sync.dma_start(
                 out=k_scales[32 * quad : 32 * quad + 4, :].bitcast(I32),
                 in_=keys_scales[0, 4 * quad : 4 * quad + 4, :].bitcast(I32),
             )
-        q_raw = sb.tile([P, PACK, Q], F32)
-        nc.sync.dma_start(out=q_raw[:], in_=query.rearrange("(p t) q -> p t q", t=PACK))
         k_words = sb.tile([P, T], U32, align_bytes=64)
         nc.sync.dma_start(out=k_words[:].bitcast(I32), in_=keys_words[0].rearrange("p n t -> p (n t)").bitcast(I32))
-        dq_raw = sb.tile([P, PACK, Q], F32)
-        nc.sync.dma_start(out=dq_raw[:], in_=dquery.rearrange("(p t) q -> p t q", t=PACK))
-        go_raw = sb.tile([P, PACK, Q], F32)
-        nc.sync.dma_start(out=go_raw[:], in_=gout.rearrange("(p t) q -> p t q", t=PACK))
         list1 = sb.tile([P, I // 16], U16)
         nc.sync.dma_start(list1[:], offs)
+        dq_raw = sb.tile([P, PACK, Q], F32)
+        nc.sync.dma_start(out=dq_raw[:], in_=dquery.rearrange("(p t) q -> p t q", t=PACK))
         list2 = sb.tile([P, I // 16], U16)
         nc.sync.dma_start(list2[:], offs2)
         v_raw = []
-        for h in range(HALVES):
-            raw = sb.tile([P, PACK, BANK], F32, tag="v_raw%d" % h, name="v_raw%d" % h)
-            nc.sync.dma_start(out=raw[:], in_=vals.rearrange("(p t) n -> p t n", t=PACK)[:, :, half(h)])
+        for n, (lo, hi) in enumerate(VAL_LOADS):
+            raw = sb.tile([P, PACK, hi - lo], F32, tag="v_raw%d" % n, name="v_raw%d" % n)
+            nc.sync.dma_start(out=raw[:], in_=vals.rearrange("(p t) n -> p t n", t=PACK)[:, :, lo:hi])
             v_raw.append(raw)
+        go_raw = sb.tile([P, PACK, Q], F32)
+        nc.sync.dma_start(out=go_raw[:], in_=gout.rearrange("(p t) q -> p t q", t=PACK))
         base_sb = sb.tile([P, T], F32)
         nc.sync.dma_start(out=base_sb[:], in_=base)
 
@@ -114,10 +115,10 @@ def tile_attend_hvborrowed_heads_kernel(tc, query, keys_words, keys_scales, gout
             for j in range(BLOCKS):
                 nc.tensor.transpose(dst[:, block(j)], src[:, block(BLOCKS * h + j)], ident[:])
 
-        q_bf = sb.tile([P, Q * PACK], BF16, align_bytes=64, tag="rows_bf")
+        q_bf = sb.tile([P, Q * PACK], BF16, align_bytes=64)
         interleave(nc.vector.tensor_copy, q_bf[:, 0 : Q_SPLIT * PACK], q_raw[:, :, 0:Q_SPLIT])
         interleave(nc.scalar.copy, q_bf[:, Q_SPLIT * PACK :], q_raw[:, :, Q_SPLIT:])
-        q_codes = sb.tile([P, Q], U32, align_bytes=64)
+        q_codes = sb.tile([P, Q], U32, align_bytes=64, tag="row_codes")
         q_scales = sb.tile([P, Q], U8, align_bytes=64)
         nc.vector.quantize_mx(out=q_codes[:].bitcast(FP8X4), scales=q_scales[:], in_=q_bf[:])
 
@@ -127,22 +128,18 @@ def tile_attend_hvborrowed_heads_kernel(tc, query, keys_words, keys_scales, gout
             cols = quarter(c)
             nc.tensor.matmul_mx(out=acc[:, 0:QUARTER], lhsT=q_codes[:].bitcast(FP8X4), lhsT_scale=q_scales[:],
                                 rhs=k_words[:, cols].bitcast(FP8X4), rhs_scale=k_scales[:, cols], start=True, stop=True)
-            if c < 3:
-                nc.scalar.copy(out=a_sb[:, cols], in_=acc[:, 0:QUARTER])
-            else:
-                nc.vector.tensor_copy(out=a_sb[:, cols], in_=acc[:, 0:QUARTER])
+            nc.vector.tensor_copy(out=a_sb[:, cols], in_=acc[:, 0:QUARTER])
 
-        dg_bf = sb.tile([P, 2 * Q * PACK], BF16, align_bytes=64, tag="rows_bf")
-        interleave(nc.vector.tensor_copy, dg_bf[:, 0 : Q * PACK], dq_raw[:])
-        interleave(nc.vector.tensor_copy, dg_bf[:, Q * PACK :], go_raw[:])
-        dg_codes = sb.tile([P, 2 * Q], U32, align_bytes=64)
-        dg_scales = sb.tile([P, 2 * Q], U8, align_bytes=64)
-        nc.vector.quantize_mx(out=dg_codes[:].bitcast(FP8X4), scales=dg_scales[:], in_=dg_bf[:])
+        dq_bf = sb.tile([P, Q * PACK], BF16, align_bytes=64)
+        interleave(nc.scalar.copy, dq_bf[:], dq_raw[:])
+        dq_codes = sb.tile([P, Q], U32, align_bytes=64, tag="row_codes")
+        dq_scales = sb.tile([P, Q], U8, align_bytes=64)
+        nc.vector.quantize_mx(out=dq_codes[:].bitcast(FP8X4), scales=dq_scales[:], in_=dq_bf[:])
 
         ta_sb = sb.tile([P, T], F32)
         for h in range(HALVES):
             acc = bank("B", h, "ta_ps")
-            nc.tensor.matmul_mx(out=acc[:], lhsT=dg_codes[:, 0:Q].bitcast(FP8X4), lhsT_scale=dg_scales[:, 0:Q],
+            nc.tensor.matmul_mx(out=acc[:], lhsT=dq_codes[:].bitcast(FP8X4), lhsT_scale=dq_scales[:],
                                 rhs=k_words[:, half(h)].bitcast(FP8X4), rhs_scale=k_scales[:, half(h)], start=True, stop=True)
             nc.scalar.copy(out=ta_sb[:, half(h)], in_=acc[:])
 
@@ -162,16 +159,16 @@ def tile_attend_hvborrowed_heads_kernel(tc, query, keys_words, keys_scales, gout
             nc.vector.tensor_tensor(a_diff[:, slots(s)], a_sb[:].indirect(list2[:, entries(s)]), a_at1[:, slots(s)], ALU.subtract)
         nc.vector.tensor_tensor(placed1[:].indirect(list1[:]), a_diff[:], share_row[:], ALU.mult)
 
-        v_bf = []
-        for h in range(HALVES):
-            grouped = sb.tile([P, BANK * PACK], BF16, align_bytes=64, name="v_bf%d" % h)
-            interleave(nc.scalar.copy, grouped[:], v_raw[h][:])
-            v_bf.append(grouped)
+        v_bf = sb.tile([P, T * PACK], BF16, align_bytes=64)
+        for raw, (lo, hi) in zip(v_raw, VAL_LOADS):
+            interleave(nc.scalar.copy, v_bf[:, lo * PACK : hi * PACK], raw[:])
+        go_bf = sb.tile([P, Q * PACK], BF16, align_bytes=64)
+        interleave(nc.scalar.copy, go_bf[:], go_raw[:])
 
         sT_ps = four_banks("CD", "sT_ps")
         for c in range(4):
             add_turned(sT_ps[c], a_sb, c, True, False)
-        sT_sb = sb.tile([P, T], F32, tag="v_raw1")
+        sT_sb = sb.tile([P, T], F32, tag="v_raw2")
         for c in range(4):
             add_turned(sT_ps[c], placed1, c, False, True)
             nc.scalar.copy(out=sT_sb[:, quarter(c)], in_=sT_ps[c][:, 0:QUARTER])
@@ -186,17 +183,20 @@ def tile_attend_hvborrowed_heads_kernel(tc, query, keys_words, keys_scales, gout
             nc.vector.tensor_copy(ta_at1[:, slots(s)], ta_sb[:].indirect(list1[:, entries(s)]))
         nc.vector.tensor_tensor(ta_diff[:, slots(0)], ta_sb[:].indirect(list2[:, entries(0)]), ta_at1[:, slots(0)], ALU.subtract)
 
+        go_codes = sb.tile([P, Q], U32, align_bytes=64)
+        go_scales = sb.tile([P, Q], U8, align_bytes=64)
+        nc.vector.quantize_mx(out=go_codes[:].bitcast(FP8X4), scales=go_scales[:], in_=go_bf[:])
         v_codes = sb.tile([P, T], U32, align_bytes=64)
         v_scales = sb.tile([P, T], U8, align_bytes=64)
         gT_sb = sb.tile([P, T], F32)
         g_ps = []
         for h in range(HALVES):
-            nc.vector.quantize_mx(out=v_codes[:, half(h)].bitcast(FP8X4), scales=v_scales[:, half(h)], in_=v_bf[h][:])
+            nc.vector.quantize_mx(out=v_codes[:, half(h)].bitcast(FP8X4), scales=v_scales[:, half(h)], in_=v_bf[:, h * BANK * PACK : (h + 1) * BANK * PACK])
             acc = bank("D", 1 - h, "c0T_ps")
             for j in range(BLOCKS):
                 cols = block(BLOCKS * h + j)
                 nc.tensor.matmul_mx(out=acc[:, block(j)], lhsT=v_codes[:, cols].bitcast(FP8X4), lhsT_scale=v_scales[:, cols],
-                                    rhs=dg_codes[:, Q:].bitcast(FP8X4), rhs_scale=dg_scales[:, Q:], start=True, stop=True)
+                                    rhs=go_codes[:].bitcast(FP8X4), rhs_scale=go_scales[:], start=True, stop=True)
             for j in range(BLOCKS):
                 c = BLOCKS * h + j
                 nc.scalar.activation(out=gT_sb[:, block(c)], in_=acc[:, block(j)], func=ACT.Copy, scale=fac_cols[:, c : c + 1])

from contextlib import ExitStack

import concourse.mybir as mybir
from concourse.masks import make_identity

D, E, T, Q, I = 512, 512, 1024, 128, 512
FLOPS = 3 * 2 * 512 * Q * T

F32 = mybir.dt.float32
BF16 = mybir.dt.bfloat16
I32 = mybir.dt.int32
U32 = mybir.dt.uint32
U16 = mybir.dt.uint16
U8 = mybir.dt.uint8
FP8X4 = mybir.dt.float8_e4m3fn_x4
ALU = mybir.AluOpType
ACT = mybir.ActivationFunctionType
AXIS_X = mybir.AxisListType.X

P = 128
PACK = 4
BANK = 512
HALVES = T // BANK
BLOCKS = BANK // P
QUARTER = T // 4
Q_SPLIT = 80
VAL_LOADS = ((0, 256), (256, 512), (512, 1024))
OUT_SCALE = 1024.0


def tile_attend_hvborrowed_heads_kernel(tc, query, keys_words, keys_scales, gout, vals, share, fac, dquery, base, offs, offs2, out):
    nc = tc.nc

    def half(h):
        return slice(h * BANK, (h + 1) * BANK)

    def quarter(c):
        return slice(c * QUARTER, (c + 1) * QUARTER)

    def slots(s):
        return slice(s * I // 2, (s + 1) * I // 2)

    def entries(s):
        return slice(s * I // 32, (s + 1) * I // 32)

    def block(j):
        return slice(j * P, (j + 1) * P)

    def interleave(copy, grouped, raw):
        copy(
            out=grouped.rearrange("p (c i t) -> p c t i", i=4, t=PACK),
            in_=raw.rearrange("p t (c i) -> p c t i", i=4),
        )

    with ExitStack() as ctx:
        sb = ctx.enter_context(tc.tile_pool(name="sb", bufs=1))
        ps = ctx.enter_context(tc.psum_pool(name="ps", bufs=1))

        def bank(role, h, name):
            return ps.tile([P, BANK], F32, tag=role + str(h), name=name + str(h))

        k_scales = sb.tile([P, T], U8, align_bytes=64)
        warm = sb.tile([P, 2], F32)
        nc.vector.memset(warm[:, 0:1], 0.0)
        nc.scalar.activation(out=warm[:, 1:2], in_=warm[:, 0:1], func=ACT.Exp)
        q_raw = sb.tile([P, PACK, Q], F32)
        nc.sync.dma_start(out=q_raw[:], in_=query.rearrange("(p t) q -> p t q", t=PACK))
        for quad in range(4):
            nc.sync.dma_start(
                out=k_scales[32 * quad : 32 * quad + 4, :].bitcast(I32),
                in_=keys_scales[0, 4 * quad : 4 * quad + 4, :].bitcast(I32),
            )
        k_words = sb.tile([P, T], U32, align_bytes=64)
        nc.sync.dma_start(out=k_words[:].bitcast(I32), in_=keys_words[0].rearrange("p n t -> p (n t)").bitcast(I32))
        list1 = sb.tile([P, I // 16], U16)
        nc.sync.dma_start(list1[:], offs)
        dq_raw = sb.tile([P, PACK, Q], F32)
        nc.sync.dma_start(out=dq_raw[:], in_=dquery.rearrange("(p t) q -> p t q", t=PACK))
        list2 = sb.tile([P, I // 16], U16)
        nc.sync.dma_start(list2[:], offs2)
        v_raw = []
        for n, (lo, hi) in enumerate(VAL_LOADS):
            raw = sb.tile([P, PACK, hi - lo], F32, tag="v_raw%d" % n, name="v_raw%d" % n)
            nc.sync.dma_start(out=raw[:], in_=vals.rearrange("(p t) n -> p t n", t=PACK)[:, :, lo:hi])
            v_raw.append(raw)
        go_raw = sb.tile([P, PACK, Q], F32)
        nc.sync.dma_start(out=go_raw[:], in_=gout.rearrange("(p t) q -> p t q", t=PACK))
        base_sb = sb.tile([P, T], F32)
        nc.sync.dma_start(out=base_sb[:], in_=base)

        fac_rows = sb.tile([P, P], F32)
        nc.gpsimd.memset(fac_rows[:], 0.0)
        nc.sync.dma_start(out=fac_rows[0 : T // P, :], in_=fac.rearrange("o (c p) -> (o c) p", p=P))
        ident = sb.tile([P, P], F32)
        make_identity(nc, ident[:])
        share_col = sb.tile([P, 1], F32)
        nc.gpsimd.dma_start(out=share_col[:], in_=share)

        placed1 = sb.tile([P, T], F32)
        placed2 = sb.tile([P, T], F32)
        nc.vector.memset(placed1[:], 0.0)
        nc.vector.memset(placed2[:], 0.0)

        def add_turned(acc, src, c, first, last):
            for j in range(2):
                nc.tensor.matmul(
                    acc[:, block(j)], lhsT=src[:, block(2 * c + j)], rhs=ident[:], is_transpose=True,
                    start=(first and j == 0), stop=(last and j == 1),
                )

        def four_banks(roles, name):
            return [bank(roles[c // 2], c % 2, name + str(c // 2)) for c in range(4)]

        def turn(dst, src, h):
            for j in range(BLOCKS):
                nc.tensor.transpose(dst[:, block(j)], src[:, block(BLOCKS * h + j)], ident[:])

        q_bf = sb.tile([P, Q * PACK], BF16, align_bytes=64)
        interleave(nc.vector.tensor_copy, q_bf[:, 0 : Q_SPLIT * PACK], q_raw[:, :, 0:Q_SPLIT])
        interleave(nc.scalar.copy, q_bf[:, Q_SPLIT * PACK :], q_raw[:, :, Q_SPLIT:])
        q_codes = sb.tile([P, Q], U32, align_bytes=64, tag="row_codes")
        q_scales = sb.tile([P, Q], U8, align_bytes=64)
        nc.vector.quantize_mx(out=q_codes[:].bitcast(FP8X4), scales=q_scales[:], in_=q_bf[:])

        a_sb = sb.tile([P, T], F32)
        for c in range(4):
            acc = bank("AD"[c // 2], c % 2, "a_ps" + str(c // 2))
            cols = quarter(c)
            nc.tensor.matmul_mx(out=acc[:, 0:QUARTER], lhsT=q_codes[:].bitcast(FP8X4), lhsT_scale=q_scales[:],
                                rhs=k_words[:, cols].bitcast(FP8X4), rhs_scale=k_scales[:, cols], start=True, stop=True)
            nc.vector.tensor_copy(out=a_sb[:, cols], in_=acc[:, 0:QUARTER])

        dq_bf = sb.tile([P, Q * PACK], BF16, align_bytes=64)
        interleave(nc.scalar.copy, dq_bf[:], dq_raw[:])
        dq_codes = sb.tile([P, Q], U32, align_bytes=64, tag="row_codes")
        dq_scales = sb.tile([P, Q], U8, align_bytes=64)
        nc.vector.quantize_mx(out=dq_codes[:].bitcast(FP8X4), scales=dq_scales[:], in_=dq_bf[:])

        ta_sb = sb.tile([P, T], F32)
        for h in range(HALVES):
            acc = bank("B", h, "ta_ps")
            nc.tensor.matmul_mx(out=acc[:], lhsT=dq_codes[:].bitcast(FP8X4), lhsT_scale=dq_scales[:],
                                rhs=k_words[:, half(h)].bitcast(FP8X4), rhs_scale=k_scales[:, half(h)], start=True, stop=True)
            nc.scalar.copy(out=ta_sb[:, half(h)], in_=acc[:])

        share_row = sb.tile([P, I], F32)
        nc.scalar.activation(out=share_row[:], in_=share_col[:].to_broadcast([P, I]), func=ACT.Copy)

        fac_ps = bank("B", 0, "fac_ps")
        nc.tensor.transpose(fac_ps[:, 0:P], fac_rows[:], ident[:])
        fac_cols = sb.tile([P, T // P], F32)
        nc.scalar.copy(out=fac_cols[:], in_=fac_ps[:, 0 : T // P])

        a_at1 = sb.tile([P, I], F32, tag="at1")
        a_diff = sb.tile([P, I], F32)
        for s in range(2):
            nc.vector.tensor_copy(a_at1[:, slots(s)], a_sb[:].indirect(list1[:, entries(s)]))
        for s in range(2):
            nc.vector.tensor_tensor(a_diff[:, slots(s)], a_sb[:].indirect(list2[:, entries(s)]), a_at1[:, slots(s)], ALU.subtract)
        nc.vector.tensor_tensor(placed1[:].indirect(list1[:]), a_diff[:], share_row[:], ALU.mult)

        v_bf = sb.tile([P, T * PACK], BF16, align_bytes=64)
        for raw, (lo, hi) in zip(v_raw, VAL_LOADS):
            interleave(nc.scalar.copy, v_bf[:, lo * PACK : hi * PACK], raw[:])
        go_bf = sb.tile([P, Q * PACK], BF16, align_bytes=64)
        interleave(nc.scalar.copy, go_bf[:], go_raw[:])

        sT_ps = four_banks("CD", "sT_ps")
        for c in range(4):
            add_turned(sT_ps[c], a_sb, c, True, False)
        sT_sb = sb.tile([P, T], F32, tag="v_raw2")
        for c in range(4):
            add_turned(sT_ps[c], placed1, c, False, True)
            nc.scalar.copy(out=sT_sb[:, quarter(c)], in_=sT_ps[c][:, 0:QUARTER])
        s_ps = [bank("A", h, "s_ps") for h in range(HALVES)]
        for h in range(HALVES):
            turn(s_ps[h], sT_sb, h)

        ta_at1 = sb.tile([P, I], F32, tag="at1")
        ta_room = sb.tile([P, I // 2 + BANK], F32)
        ta_diff = ta_room[:, 0:I]
        for s in range(2):
            nc.vector.tensor_copy(ta_at1[:, slots(s)], ta_sb[:].indirect(list1[:, entries(s)]))
        nc.vector.tensor_tensor(ta_diff[:, slots(0)], ta_sb[:].indirect(list2[:, entries(0)]), ta_at1[:, slots(0)], ALU.subtract)

        go_codes = sb.tile([P, Q], U32, align_bytes=64)
        go_scales = sb.tile([P, Q], U8, align_bytes=64)
        nc.vector.quantize_mx(out=go_codes[:].bitcast(FP8X4), scales=go_scales[:], in_=go_bf[:])
        v_codes = sb.tile([P, T], U32, align_bytes=64)
        v_scales = sb.tile([P, T], U8, align_bytes=64)
        gT_sb = sb.tile([P, T], F32)
        g_ps = []
        for h in range(HALVES):
            nc.vector.quantize_mx(out=v_codes[:, half(h)].bitcast(FP8X4), scales=v_scales[:, half(h)], in_=v_bf[:, h * BANK * PACK : (h + 1) * BANK * PACK])
            acc = bank("D", 1 - h, "c0T_ps")
            for j in range(BLOCKS):
                cols = block(BLOCKS * h + j)
                nc.tensor.matmul_mx(out=acc[:, block(j)], lhsT=v_codes[:, cols].bitcast(FP8X4), lhsT_scale=v_scales[:, cols],
                                    rhs=go_codes[:].bitcast(FP8X4), rhs_scale=go_scales[:], start=True, stop=True)
            for j in range(BLOCKS):
                c = BLOCKS * h + j
                nc.scalar.activation(out=gT_sb[:, block(c)], in_=acc[:, block(j)], func=ACT.Copy, scale=fac_cols[:, c : c + 1])
            g_h = bank("D", 1 - h, "g_ps")
            turn(g_h, gT_sb, h)
            g_ps.append(g_h)

        neg_s1 = sb.tile([P, BANK], F32)
        neg_max_half = sb.tile([P, 1], F32)
        neg_max = sb.tile([P, 1], F32)
        nc.vector.tensor_scalar(out=ta_room[:, I // 2 :], in0=s_ps[0][:], scalar1=-1.0, scalar2=None,
                                op0=ALU.mult, op1=ALU.min, accum_out=neg_max_half[:])
        nc.vector.tensor_tensor(ta_diff[:, slots(1)], ta_sb[:].indirect(list2[:, entries(1)]), ta_at1[:, slots(1)], ALU.subtract)
        nc.vector.tensor_scalar(out=neg_s1[:], in0=s_ps[1][:], scalar1=-1.0, scalar2=neg_max_half[:],
                                op0=ALU.mult, op1=ALU.min, accum_out=neg_max[:])
        p = sb.tile([P, T], F32)
        z_halves = sb.tile([P, HALVES], F32)
        for h in range(HALVES):
            nc.scalar.activation(out=p[:, half(h)], in_=s_ps[h][:], func=ACT.Exp, bias=neg_max[:], accum_out=z_halves[:, h : h + 1])
        z = sb.tile([P, 2], F32)
        z_parts = sb.tile([P, 2, HALVES], F32)
        for c, scale in enumerate((1.0, -1.0 / OUT_SCALE)):
            nc.scalar.activation(out=z_parts[:, c, :], in_=z_halves[:], func=ACT.Copy, scale=scale, accum_out=z[:, c : c + 1])

        nc.vector.tensor_tensor(placed1[:].indirect(list1[:]), ta_diff, share_row[:], ALU.mult)
        xs = sb.tile([P, T], F32)
        for h in range(HALVES):
            nc.gpsimd.tensor_tensor(out=xs[:, half(h)], in0=ta_sb[:, half(h)], in1=placed1[:, half(h)], op=ALU.add)

        inv = sb.tile([P, 2], F32)
        nc.vector.reciprocal(out=inv[:], in_=z[:])
        r, neg_k = inv[:, 0:1], inv[:, 1:2]
        pk_room = sb.tile([P, BANK + T], F32)
        neg_pk = pk_room[:, BANK:]
        for h in range(HALVES):
            nc.scalar.activation(out=neg_pk[:, half(h)], in_=p[:, half(h)], func=ACT.Copy, scale=neg_k)
        prob = sb.tile([P, T], F32)
        nc.scalar.activation(out=prob[:], in_=p[:], func=ACT.Copy, scale=r)

        gp = sb.tile([P, T], F32)
        g_mean_halves = sb.tile([P, HALVES], F32)
        for h in range(HALVES):
            nc.vector.scalar_tensor_tensor(out=gp[:, half(h)], in0=g_ps[h][:], scalar=1.0, in1=p[:, half(h)],
                                           op0=ALU.mult, op1=ALU.mult, accum_out=g_mean_halves[:, h : h + 1])
        g_mean = sb.tile([P, 1], F32)
        g_mean_parts = sb.tile([P, HALVES], F32)
        nc.vector.tensor_scalar(out=g_mean_parts[:], in0=g_mean_halves[:], scalar1=r, scalar2=None, op0=ALU.mult, op1=ALU.add, accum_out=g_mean[:])
        centred = sb.tile([P, T], F32)
        for h in range(HALVES):
            nc.vector.scalar_tensor_tensor(out=centred[:, half(h)], in0=g_ps[h][:], scalar=g_mean[:], in1=neg_pk[:, half(h)],
                                           op0=ALU.subtract, op1=ALU.mult)
        xs_mean = sb.tile([P, 1], F32)
        nc.vector.scalar_tensor_tensor(out=pk_room[:, 0:T], in0=xs[:], scalar=r, in1=p[:], op0=ALU.mult, op1=ALU.mult, accum_out=xs_mean[:])
        both = sb.tile([P, T], F32)
        both_sum = sb.tile([P, 1], F32)
        nc.vector.scalar_tensor_tensor(out=both[:], in0=xs[:], scalar=xs_mean[:], in1=centred[:],
                                       op0=ALU.subtract, op1=ALU.mult, accum_out=both_sum[:])
        xds = sb.tile([P, T], F32)
        nc.vector.scalar_tensor_tensor(out=xds[:], in0=prob[:], scalar=both_sum[:], in1=both[:], op0=ALU.mult, op1=ALU.subtract)

        uT_ps = four_banks("BA", "uT_ps")
        for c in range(4):
            add_turned(uT_ps[c], base_sb, c, True, False)
        xe1 = sb.tile([P, I], F32)
        nc.vector.tensor_tensor(xe1[:], xds[:].indirect(list1[:]), share_row[:], ALU.mult)
        for c in range(4):
            add_turned(uT_ps[c], xds, c, False, False)
        nc.vector.tensor_copy(placed2[:].indirect(list2[:]), xe1[:])
        xe2 = sb.tile([P, I], F32)
        nc.scalar.activation(out=xe2[:], in_=xe1[:], func=ACT.Copy, scale=-1.0)
        uT_sb = sb.tile([P, T], F32)
        for c in range(4):
            add_turned(uT_ps[c], placed2, c, False, True)
            nc.scalar.copy(out=uT_sb[:, quarter(c)], in_=uT_ps[c][:, 0:QUARTER])
        u_ps = [bank("C", h, "u_ps") for h in range(HALVES)]
        for h in range(HALVES):
            turn(u_ps[h], uT_sb, h)
        nc.vector.tensor_copy(placed1[:].indirect(list1[:]), xe2[:])
        result = sb.tile([P, T], F32)
        for c in range(4):
            nc.vector.tensor_tensor(out=result[:, quarter(c)], in0=u_ps[c // 2][:, quarter(c % 2)], in1=placed1[:, quarter(c)], op=ALU.add)
            (nc.sync if c % 2 == 0 else nc.scalar).dma_start(out=out[:, quarter(c)], in_=result[:, quarter(c)])
